import numpy as np, ml_dtypes
CORES = [0,8,16,24,32,40,48,56,64,72,80,88,96,104,112,120]
N = 16
ROWS, COLS = 4, 4
def setup_inputs(rng):
    return {"x": rng.standard_normal((N, 128, 8), dtype=np.float32).astype(ml_dtypes.bfloat16)}
def reference(x):
    g = x.astype(np.float64).reshape(ROWS, COLS, 128, 8)
    rs = g.sum(axis=1)
    cs = g.sum(axis=0)
    y1 = np.stack([rs[r // COLS] for r in range(N)]).astype(x.dtype)
    y2 = np.stack([cs[r % COLS] for r in range(N)]).astype(x.dtype)
    return {"y1": y1, "y2": y2}

@@ -1,0 +1,65 @@
+from concourse.bass import DstId, RemoteDMATransfer
+from concourse.mybir import AluOpType
+
+BF = "bfloat16"
+SCRATCH = {
+    "xs": ("dram", [128, 8], BF),
+    "peer": ("dram", [128, 8], BF),
+    "rowp": ("dram", [128, 8], BF),
+    "cols": ("dram", [128, 8], BF),
+    "hx": ("dram", [5, 128, 8], BF),
+}
+SEMAPHORES = ["loaded", "init", "sent", "peer_in", "rowp_in", "col_in", "acc", "stored", "harr", "hsent"]
+
+HELPER = 2
+M_A = 0x0003
+M_B = 0x000C
+M_C = 0x00F0
+M_D = 0x0F00
+M_ROW = 0x000F
+
+
+def _dst(topo, core):
+    rid, pid, _se = topo.addr(core)
+    return DstId(rid=rid, pnc=pid)
+
+
+def rank_program(g, core, T, topo):
+    k, c = divmod(core, 8)
+    S = T.sem
+    if c == 0:
+        g.sync.dma_start(T.xs[:], T.x[:]).then_inc(S.loaded, 16)
+        g.scalar.dma_start(T.y1[:], T.x[:]).then_inc(S.init, 16)
+        col = [s for s in range(k % 4, 16, 4) if s != k]
+        g.wait_ge(S.loaded, 16)
+        g.remote_dma_fused([
+            RemoteDMATransfer(dst_ids=[_dst(topo, 8 * (k ^ 2) + HELPER)], dma_engine_mask=M_A, remote_sem=S.harr,
+                              src=T.xs[:], dst=T.hx[1]),
+            RemoteDMATransfer(dst_ids=[_dst(topo, 8 * k + HELPER)], dma_engine_mask=M_D, remote_sem=S.harr,
+                              src=T.xs[:], dst=T.hx[0]),
+            RemoteDMATransfer(dst_ids=[_dst(topo, 8 * (k ^ 2))], dma_engine_mask=M_B, remote_sem=S.peer_in,
+                              src=T.xs[:], dst=T.peer[:]),
+            RemoteDMATransfer(dst_ids=[_dst(topo, 8 * s + HELPER) for s in col], dma_engine_mask=M_C,
+                              remote_sem=S.harr, srcs=[T.xs[:]],
+                              dsts=[T.hx[2 + (k // 4 - s // 4) % 4 - 1] for s in col]),
+        ], local_sem=S.sent)
+        g.sync.wait_ge(S.col_in, 4)
+        g.sync.dma_start(T.y2[:], T.cols[:]).then_inc(S.stored, 16)
+        g.wait_ge(S.init, 16)
+        g.wait_ge(S.peer_in, 2)
+        g.dma_start(T.y1[:], T.peer[:], accum_op=AluOpType.add).then_inc(S.acc, 16)
+        g.wait_ge(S.acc, 16)
+        g.wait_ge(S.rowp_in, 4)
+        g.dma_start(T.y1[:], T.rowp[:], accum_op=AluOpType.add).then_inc(S.acc, 16)
+        g.wait_ge(S.acc, 32)
+        g.wait_ge(S.sent, 2 + 4 + 2 + 4)
+        g.wait_ge(S.stored, 16)
+    elif c == HELPER:
+        g.wait_ge(S.harr, 2 + 4 + 3 * 4)
+        g.remote_dma_fused([
+            RemoteDMATransfer(dst_ids=[_dst(topo, 8 * (k ^ 1))], dma_engine_mask=M_ROW, remote_sem=S.rowp_in,
+                              srcs=[T.hx[0], T.hx[1]], dsts=[T.rowp[:]], alu_op=1),
+            RemoteDMATransfer(dst_ids=[_dst(topo, 8 * k)], dma_engine_mask=M_D, remote_sem=S.col_in,
+                              srcs=[T.hx[0], T.hx[2], T.hx[3], T.hx[4]], dsts=[T.cols[:]], alu_op=1),
+        ], local_sem=S.hsent)
+        g.wait_ge(S.hsent, 8)

@@ -1,22 +1,22 @@
 from concourse.bass import DstId, RemoteDMATransfer
-from concourse.mybir import AluOpType
 
 BF = "bfloat16"
 SCRATCH = {
     "xs": ("dram", [128, 8], BF),
-    "peer": ("dram", [128, 8], BF),
-    "rowp": ("dram", [128, 8], BF),
+    "rows": ("dram", [128, 8], BF),
     "cols": ("dram", [128, 8], BF),
-    "hx": ("dram", [5, 128, 8], BF),
+    "hx": ("dram", [4, 128, 8], BF),
 }
-SEMAPHORES = ["loaded", "init", "sent", "peer_in", "rowp_in", "col_in", "acc", "stored", "harr", "hsent"]
+SEMAPHORES = ["loaded", "sent", "row_in", "col_in", "stored", "harr", "hpart", "hsent"]
 
-HELPER = 2
-M_A = 0x0003
-M_B = 0x000C
+ROWH = 2
+COLH = 3
+M_A = 0x000F
 M_C = 0x00F0
 M_D = 0x0F00
-M_ROW = 0x000F
+M_E = 0xF000
+M_LO = 0x00FF
+M_HI = 0xFF00
 
 
 def _dst(topo, core):
@@ -29,37 +29,41 @@ def rank_program(g, core, T, topo):
     S = T.sem
     if c == 0:
         g.sync.dma_start(T.xs[:], T.x[:]).then_inc(S.loaded, 16)
-        g.scalar.dma_start(T.y1[:], T.x[:]).then_inc(S.init, 16)
         col = [s for s in range(k % 4, 16, 4) if s != k]
         g.wait_ge(S.loaded, 16)
         g.remote_dma_fused([
-            RemoteDMATransfer(dst_ids=[_dst(topo, 8 * (k ^ 2) + HELPER)], dma_engine_mask=M_A, remote_sem=S.harr,
+            RemoteDMATransfer(dst_ids=[_dst(topo, 8 * (k ^ 2) + ROWH)], dma_engine_mask=M_A, remote_sem=S.harr,
                               src=T.xs[:], dst=T.hx[1]),
-            RemoteDMATransfer(dst_ids=[_dst(topo, 8 * k + HELPER)], dma_engine_mask=M_D, remote_sem=S.harr,
+            RemoteDMATransfer(dst_ids=[_dst(topo, 8 * k + ROWH)], dma_engine_mask=M_D, remote_sem=S.harr,
                               src=T.xs[:], dst=T.hx[0]),
-            RemoteDMATransfer(dst_ids=[_dst(topo, 8 * (k ^ 2))], dma_engine_mask=M_B, remote_sem=S.peer_in,
-                              src=T.xs[:], dst=T.peer[:]),
-            RemoteDMATransfer(dst_ids=[_dst(topo, 8 * s + HELPER) for s in col], dma_engine_mask=M_C,
+            RemoteDMATransfer(dst_ids=[_dst(topo, 8 * s + COLH) for s in col], dma_engine_mask=M_C,
                               remote_sem=S.harr, srcs=[T.xs[:]],
-                              dsts=[T.hx[2 + (k // 4 - s // 4) % 4 - 1] for s in col]),
+                              dsts=[T.hx[(k // 4 - s // 4) % 4] for s in col]),
+            RemoteDMATransfer(dst_ids=[_dst(topo, 8 * k + COLH)], dma_engine_mask=M_E, remote_sem=S.harr,
+                              src=T.xs[:], dst=T.hx[0]),
         ], local_sem=S.sent)
-        g.sync.wait_ge(S.col_in, 4)
-        g.sync.dma_start(T.y2[:], T.cols[:]).then_inc(S.stored, 16)
-        g.wait_ge(S.init, 16)
-        g.wait_ge(S.peer_in, 2)
-        g.dma_start(T.y1[:], T.peer[:], accum_op=AluOpType.add).then_inc(S.acc, 16)
-        g.wait_ge(S.acc, 16)
-        g.wait_ge(S.rowp_in, 4)
-        g.dma_start(T.y1[:], T.rowp[:], accum_op=AluOpType.add).then_inc(S.acc, 16)
-        g.wait_ge(S.acc, 32)
-        g.wait_ge(S.sent, 2 + 4 + 2 + 4)
-        g.wait_ge(S.stored, 16)
-    elif c == HELPER:
-        g.wait_ge(S.harr, 2 + 4 + 3 * 4)
+        g.scalar.wait_ge(S.col_in, 8)
+        g.scalar.dma_start(T.y2[:], T.cols[:]).then_inc(S.stored, 16)
+        g.sync.wait_ge(S.row_in, 8)
+        g.sync.dma_start(T.y1[:], T.rows[:]).then_inc(S.stored, 16)
+        g.wait_ge(S.sent, 16)
+        g.wait_ge(S.stored, 32)
+    elif c == ROWH:
+        g.wait_ge(S.harr, 4 + 4)
         g.remote_dma_fused([
-            RemoteDMATransfer(dst_ids=[_dst(topo, 8 * (k ^ 1))], dma_engine_mask=M_ROW, remote_sem=S.rowp_in,
-                              srcs=[T.hx[0], T.hx[1]], dsts=[T.rowp[:]], alu_op=1),
-            RemoteDMATransfer(dst_ids=[_dst(topo, 8 * k)], dma_engine_mask=M_D, remote_sem=S.col_in,
-                              srcs=[T.hx[0], T.hx[2], T.hx[3], T.hx[4]], dsts=[T.cols[:]], alu_op=1),
+            RemoteDMATransfer(dst_ids=[_dst(topo, 8 * (k ^ 1) + ROWH)], dma_engine_mask=M_LO, remote_sem=S.hpart,
+                              srcs=[T.hx[0], T.hx[1]], dsts=[T.hx[2]], alu_op=1),
+        ], local_sem=S.hsent)
+        g.wait_ge(S.hpart, 8)
+        g.remote_dma_fused([
+            RemoteDMATransfer(dst_ids=[_dst(topo, 8 * k)], dma_engine_mask=M_HI, remote_sem=S.row_in,
+                              srcs=[T.hx[0], T.hx[1], T.hx[2]], dsts=[T.rows[:]], alu_op=1),
+        ], local_sem=S.hsent)
+        g.wait_ge(S.hsent, 16)
+    elif c == COLH:
+        g.wait_ge(S.harr, 4 + 3 * 4)
+        g.remote_dma_fused([
+            RemoteDMATransfer(dst_ids=[_dst(topo, 8 * k)], dma_engine_mask=M_HI, remote_sem=S.col_in,
+                              srcs=[T.hx[0], T.hx[1], T.hx[2], T.hx[3]], dsts=[T.cols[:]], alu_op=1),
         ], local_sem=S.hsent)
         g.wait_ge(S.hsent, 8)

from concourse.bass import DstId, RemoteDMATransfer

BF = "bfloat16"
SCRATCH = {
    "xs": ("dram", [128, 8], BF),
    "rows": ("dram", [128, 8], BF),
    "cols": ("dram", [128, 8], BF),
    "hx": ("dram", [4, 128, 8], BF),
}
SEMAPHORES = ["loaded", "sent", "row_in", "col_in", "stored", "harr", "hpart", "hsent"]

ROWH = 2
COLH = 3
M_A = 0x000F
M_C = 0x00F0
M_D = 0x0F00
M_E = 0xF000
M_LO = 0x00FF
M_HI = 0xFF00


def _dst(topo, core):
    rid, pid, _se = topo.addr(core)
    return DstId(rid=rid, pnc=pid)


def rank_program(g, core, T, topo):
    k, c = divmod(core, 8)
    S = T.sem
    if c == 0:
        g.sync.dma_start(T.xs[:], T.x[:]).then_inc(S.loaded, 16)
        col = [s for s in range(k % 4, 16, 4) if s != k]
        g.wait_ge(S.loaded, 16)
        g.remote_dma_fused([
            RemoteDMATransfer(dst_ids=[_dst(topo, 8 * (k ^ 2) + ROWH)], dma_engine_mask=M_A, remote_sem=S.harr,
                              src=T.xs[:], dst=T.hx[1]),
            RemoteDMATransfer(dst_ids=[_dst(topo, 8 * k + ROWH)], dma_engine_mask=M_D, remote_sem=S.harr,
                              src=T.xs[:], dst=T.hx[0]),
            RemoteDMATransfer(dst_ids=[_dst(topo, 8 * s + COLH) for s in col], dma_engine_mask=M_C,
                              remote_sem=S.harr, srcs=[T.xs[:]],
                              dsts=[T.hx[(k // 4 - s // 4) % 4] for s in col]),
            RemoteDMATransfer(dst_ids=[_dst(topo, 8 * k + COLH)], dma_engine_mask=M_E, remote_sem=S.harr,
                              src=T.xs[:], dst=T.hx[0]),
        ], local_sem=S.sent)
        g.scalar.wait_ge(S.col_in, 8)
        g.scalar.dma_start(T.y2[:], T.cols[:]).then_inc(S.stored, 16)
        g.sync.wait_ge(S.row_in, 8)
        g.sync.dma_start(T.y1[:], T.rows[:]).then_inc(S.stored, 16)
        g.wait_ge(S.sent, 16)
        g.wait_ge(S.stored, 32)
    elif c == ROWH:
        g.wait_ge(S.harr, 4 + 4)
        g.remote_dma_fused([
            RemoteDMATransfer(dst_ids=[_dst(topo, 8 * (k ^ 1) + ROWH)], dma_engine_mask=M_LO, remote_sem=S.hpart,
                              srcs=[T.hx[0], T.hx[1]], dsts=[T.hx[2]], alu_op=1),
        ], local_sem=S.hsent)
        g.wait_ge(S.hpart, 8)
        g.remote_dma_fused([
            RemoteDMATransfer(dst_ids=[_dst(topo, 8 * k)], dma_engine_mask=M_HI, remote_sem=S.row_in,
                              srcs=[T.hx[0], T.hx[1], T.hx[2]], dsts=[T.rows[:]], alu_op=1),
        ], local_sem=S.hsent)
        g.wait_ge(S.hsent, 16)
    elif c == COLH:
        g.wait_ge(S.harr, 4 + 3 * 4)
        g.remote_dma_fused([
            RemoteDMATransfer(dst_ids=[_dst(topo, 8 * k)], dma_engine_mask=M_HI, remote_sem=S.col_in,
                              srcs=[T.hx[0], T.hx[1], T.hx[2], T.hx[3]], dsts=[T.cols[:]], alu_op=1),
        ], local_sem=S.hsent)
        g.wait_ge(S.hsent, 8)
